import numpy as np
import ml_dtypes


def mxq(x, axis, fmt="e4m3"):
    dtype, down = {"e4m3": (ml_dtypes.float8_e4m3fn, 7), "e5m2": (ml_dtypes.float8_e5m2, 14)}[fmt]
    v = np.moveaxis(np.asarray(x, np.float32).astype(ml_dtypes.bfloat16).astype(np.float64), axis, -1)
    blocks = v.reshape(v.shape[:-1] + (-1, 32))
    amax = np.abs(blocks).max(-1, keepdims=True)
    byte = np.maximum(np.where(amax > 0, np.frexp(amax)[1] - 1 + 127, 0) - down, 1)
    scale = np.exp2(byte - 127.0)
    codes = (blocks / scale).astype(np.float32).astype(dtype).astype(np.float64)
    return np.moveaxis((codes * scale).reshape(v.shape), -1, axis)


WIDE = False


def mx_kscale(k):
    if not WIDE:
        return np.ones(k)
    levels = np.array([10, -10, 5, -5, 0])
    if k % 512:
        return np.exp2(np.random.permutation(np.resize(levels, k // 32))).repeat(32)
    a = np.empty((k // 512, 16))
    for p in range(k // 512):
        a[p, :8] = np.random.permutation(np.resize(levels, 8))
        for g in range(8):
            far = levels[np.abs(levels - a[p, g]) >= 10]
            a[p, g + 8] = far[np.random.randint(len(far))]
    return np.exp2(a.ravel()).repeat(32)


def f64(x):
    return np.asarray(x).astype(np.float64)


def striped(idx):
    return np.tile(idx.reshape(-1, 16).T, (8, 1)).astype(np.uint16)


def unstriped(offs):
    return offs[:16].T.reshape(-1).astype(np.int64)


def silu(v):
    return v / (1.0 + np.exp(-np.maximum(v, -700.0)))


def d_silu(v):
    s = 1.0 / (1.0 + np.exp(-np.maximum(v, -700.0)))
    return s * (1.0 + v * (1.0 - s))


K, T, E, C, H, N = 384, 2048, 8, 128, 512, 512


def by_expert(wq, xq):
    return np.concatenate([wq[e].T @ xq[:, e * C:(e + 1) * C] for e in range(E)], axis=1)


def setup_inputs():
    n = np.random.standard_normal
    s = mx_kscale(N)[:, None]
    u = mx_kscale(H)
    return {
        "dyT": (n((N, T)) * s).astype(np.float32),
        "a1": n((H, E * C)).astype(np.float32),
        "a3": n((H, E * C)).astype(np.float32),
        "w2": (n((E, N, H)) / np.sqrt(N) / s[None] * u[None, None, :]).astype(np.float32),
        "w1": (n((E, H, K)) / np.sqrt(H) / u[None, :, None]).astype(np.float32),
        "w3": (n((E, H, K)) / np.sqrt(H) / u[None, :, None]).astype(np.float32),
        "gate": np.tile(np.random.uniform(0.2, 1.0, E * C), (N, 1)).astype(np.float32),
        "offs": striped(np.random.permutation(T)[:E * C]),
    }


def reference(dyT, a1, a3, w2, w1, w3, gate, offs):
    idx = unstriped(offs)
    gq = mxq(f64(gate) * f64(dyT)[:, idx], 0, "e4m3")
    dh = by_expert(mxq(f64(w2), 1, "e4m3"), gq)
    da1 = dh * f64(a3) * d_silu(f64(a1))
    da3 = dh * silu(f64(a1))
    dx = by_expert(mxq(f64(w1), 1, "e4m3"), mxq(da1, 0, "e4m3")) + by_expert(mxq(f64(w3), 1, "e4m3"), mxq(da3, 0, "e4m3"))
    out = np.zeros((K, T))
    out[:, idx] = dx
    return out

@@ -1,0 +1,199 @@
+from contextlib import ExitStack
+
+import concourse.mybir as mybir
+
+N, T, H, K = 512, 2048, 512, 384
+E, C = 8, 128
+S = E * C
+
+F32 = mybir.dt.float32
+BF16 = mybir.dt.bfloat16
+U32 = mybir.dt.uint32
+U16 = mybir.dt.uint16
+U8 = mybir.dt.uint8
+FP8X4 = mybir.dt.float8_e4m3fn_x4
+ADD = mybir.AluOpType.add
+SUB = mybir.AluOpType.subtract
+MULT = mybir.AluOpType.mult
+SILU = mybir.ActivationFunctionType.Silu
+TANH = mybir.ActivationFunctionType.Tanh
+
+FLOPS = 2 * S * H * N + 2 * 2 * S * H * K
+BYTES = 4 * (N * T + 2 * H * S + E * N * H + 2 * E * H * K + S + K * T) + 2 * S
+
+P = 128
+J = 4
+PAIR = 2 * C
+KT = K // P
+RAW_BUFS = 9
+ON_VECTOR = {("w2", 1), ("w3", 0), ("w3", 1), ("w3", 3), ("w3", 5), ("w3", 7)}
+
+
+def tile_moe_bdx_glu_silu_kernel(tc, dyT, a1, a3, w2, w1, w3, gate, offs, out):
+    nc = tc.nc
+    with ExitStack() as ctx:
+        keep = ctx.enter_context(tc.tile_pool(name="keep", bufs=1))
+        raws = ctx.enter_context(tc.tile_pool(name="raws", bufs=RAW_BUFS))
+        work = ctx.enter_context(tc.tile_pool(name="work", bufs=2))
+        more = ctx.enter_context(tc.tile_pool(name="more", bufs=4))
+        psum = ctx.enter_context(tc.psum_pool(name="psum", bufs=4))
+
+        offsets = keep.tile([P, S // 16], U16, name="offsets")
+        nc.sync.dma_start(offsets[:], offs)
+
+        warm = keep.tile([P, 1], F32, name="warm")
+        nc.vector.memset(warm[:], 0.0)
+        nc.scalar.activation(warm[:], warm[:], SILU)
+
+        gate_t = keep.tile([P, S], F32, name="gate_t")
+        lt = [keep.tile([P, J, PAIR], F32, name=f"l{q}") for q in range(4)]
+        yt = [keep.tile([P, J, PAIR], F32, name=f"y{q}") for q in range(4)]
+        win = [keep.tile([P, T], F32, name=f"win{k}") for k in range(KT)]
+        g32 = keep.tile([P, J, S], F32, name="g32")
+        gq = keep.tile([P, S], U32, name="gq", align_bytes=64)
+        gs = keep.tile([P, S], U8, name="gs", align_bytes=64)
+        for k in range(KT):
+            nc.gpsimd.memset(win[k][:], 0.0)
+
+        order = [("a1", 0), ("gate", 0), ("a3", 0), ("dy", 0), ("a1", 1), ("dy", 1), ("a3", 1), ("w2", 0), ("dy", 2),
+                 ("a1", 2), ("dy", 3), ("w2", 1), ("a3", 2), ("w1", 0), ("w3", 0), ("w2", 2), ("w1", 1), ("w3", 1),
+                 ("a1", 3), ("a3", 3), ("w2", 3)]
+        for e in range(2, E):
+            order += [("w1", e), ("w3", e)]
+            if e + 2 < E:
+                order.append(("w2", e + 2))
+        source = {
+            "a1": lambda q: a1.rearrange("(p r) n -> p r n", r=J)[:, :, q * PAIR : (q + 1) * PAIR],
+            "a3": lambda q: a3.rearrange("(p r) n -> p r n", r=J)[:, :, q * PAIR : (q + 1) * PAIR],
+            "gate": lambda q: gate[0:P, :],
+            "dy": lambda j: dyT.rearrange("(p j) t -> p j t", j=J)[:, j, :],
+            "w2": lambda e: w2[e].rearrange("(p j) i -> p j i", j=J),
+            "w1": lambda e: w1[e].rearrange("(p j) k -> p j k", j=J),
+            "w3": lambda e: w3[e].rearrange("(p j) k -> p j k", j=J),
+        }
+        ringed = {}
+        pending = list(order)
+
+        def load():
+            while pending and len(ringed) < RAW_BUFS:
+                kind, x = pending[0]
+                pending.remove(pending[0])
+                if kind == "a1":
+                    dst = lt[x]
+                elif kind == "a3":
+                    dst = yt[x]
+                elif kind == "gate":
+                    dst = gate_t
+                else:
+                    shape = {"dy": [P, T], "w2": [P, J, H], "w1": [P, J, K], "w3": [P, J, K]}[kind]
+                    dst = raws.tile(shape, F32, name="raw", tag="raw")
+                    ringed[(kind, x)] = dst
+                nc.sync.dma_start(dst[:], source[kind](x))
+
+        def take(kind, x):
+            return ringed.pop((kind, x))
+
+        def cast(job, dst, src):
+            if job in ON_VECTOR:
+                nc.vector.tensor_copy(dst, src)
+            else:
+                nc.scalar.copy(dst, src)
+
+        def quantize(codes, scales, grouped):
+            nc.vector.quantize_mx(codes.bitcast(FP8X4), scales, grouped)
+
+        def matmul(dst, lq, ls, m, rq, rs, n, start, stop):
+            nc.tensor.matmul_mx(dst, lq[:, m].bitcast(FP8X4), ls[:, m], rq[:, n].bitcast(FP8X4), rs[:, n], start=start, stop=stop)
+
+        def act(q):
+            th = work.tile([P, J, PAIR], F32, name="th")
+            ng = work.tile([P, J, PAIR], F32, name="ng")
+            nc.scalar.activation(th[:], lt[q][:], TANH, scale=0.5)
+            nc.scalar.activation(ng[:], lt[q][:], SILU, scale=-1.0)
+            nc.scalar.activation(lt[q][:], lt[q][:], SILU)
+            nc.vector.scalar_tensor_tensor(yt[q][:], th[:], 1.0, yt[q][:], ADD, MULT)
+            nc.vector.scalar_tensor_tensor(yt[q][:], ng[:], 1.0, yt[q][:], SUB, MULT)
+
+        def gather(j):
+            window = take("dy", j)
+            nc.vector.tensor_tensor(g32[:, j, :], window[:].indirect(offsets[:]), gate_t[:], MULT)
+
+        def quantize_g(q):
+            cols = slice(q * PAIR, (q + 1) * PAIR)
+            gb = work.tile([P, PAIR, J], BF16, name="gb", align_bytes=64)
+            cast(("g", q), gb[:].rearrange("p (c i) j -> p c j i", i=4), g32[:, :, cols].rearrange("p j (c i) -> p c j i", i=4))
+            quantize(gq[:, cols], gs[:, cols], gb[:].rearrange("p n j -> p (n j)"))
+
+        w2_ready = {}
+        da_ready = {}
+        dx_ready = {}
+
+        def make_w2(e):
+            raw = take("w2", e)
+            wb = work.tile([P, J * H], BF16, name="w2b", align_bytes=64)
+            wq = work.tile([P, H], U32, name="w2q", align_bytes=64)
+            ws = work.tile([P, H], U8, name="w2s", align_bytes=64)
+            cast(("w2", e), wb[:].rearrange("p (t m j) -> p m j t", t=4, j=J), raw[:].rearrange("p j (m t) -> p m j t", t=4))
+            quantize(wq[:], ws[:], wb[:])
+            w2_ready[e] = (wq, ws)
+
+        def first_product(e):
+            wq, ws = w2_ready.pop(e)
+            dh = psum.tile([P, J, C], F32, name="dh")
+            for t in range(J):
+                matmul(dh[:, t, :], wq, ws, slice(t * P, (t + 1) * P), gq, gs, slice(e * C, (e + 1) * C), True, True)
+            db = work.tile([P, 2, C, J], BF16, name="db", align_bytes=64)
+            dq = more.tile([P, 2 * C], U32, name="dq", align_bytes=64)
+            ds = more.tile([P, 2 * C], U8, name="ds", align_bytes=64)
+            sub = slice((e % 2) * C, (e % 2 + 1) * C)
+            dhv = dh[:].rearrange("p r n -> p n r")
+            nc.vector.scalar_tensor_tensor(db[:, 0, :, :], dhv, -0.5, yt[e // 2][:, :, sub].rearrange("p r n -> p n r"), MULT, MULT)
+            nc.vector.tensor_tensor(db[:, 1, :, :], dhv, lt[e // 2][:, :, sub].rearrange("p r n -> p n r"), MULT)
+            quantize(dq[:], ds[:], db[:].rearrange("p a n r -> p (a n r)"))
+            da_ready[e] = (dq, ds)
+
+        def second_product(e):
+            wb = work.tile([P, 2 * K, J], BF16, name="wb", align_bytes=64)
+            wq = work.tile([P, 2 * K], U32, name="wq", align_bytes=64)
+            ws = work.tile([P, 2 * K], U8, name="ws", align_bytes=64)
+            for a, kind in enumerate(("w1", "w3")):
+                raw = take(kind, e)
+                cast((kind, e), wb[:, a * K : (a + 1) * K, :].rearrange("p (c i) j -> p c j i", i=4), raw[:].rearrange("p j (c i) -> p c j i", i=4))
+            for lo, hi in ((0, 512), (512, 768)):
+                quantize(wq[:, lo:hi], ws[:, lo:hi], wb[:, lo:hi, :].rearrange("p n j -> p (n j)"))
+            dq, ds = da_ready.pop(e)
+            dx = psum.tile([P, KT, C], F32, name="dx")
+            for k in range(KT):
+                for a in range(2):
+                    m = slice(a * K + k * P, a * K + (k + 1) * P)
+                    matmul(dx[:, k, :], wq, ws, m, dq, ds, slice(a * C, (a + 1) * C), a == 0, a == 1)
+            if e % 2 == 0:
+                dxs = more.tile([P, KT, PAIR], F32, name="dxs")
+                dx_ready[e // 2] = dxs
+            nc.scalar.copy(dx_ready[e // 2][:, :, (e % 2) * C : (e % 2 + 1) * C], dx[:])
+
+        def scatter(pair, k):
+            cols = slice(pair * PAIR // 16, (pair + 1) * PAIR // 16)
+            nc.vector.tensor_copy(win[k][:].indirect(offsets[:, cols]), dx_ready[pair][:, k, :])
+
+        steps = [(act, 0), (gather, 0), (gather, 1), (act, 1), (make_w2, 0), (gather, 2), (gather, 3), (act, 2),
+                 (make_w2, 1), (quantize_g, 0), (first_product, 0), (first_product, 1), (quantize_g, 1)]
+        for e in range(E):
+            steps.append((second_product, e))
+            if e + 2 < E:
+                steps.append((make_w2, e + 2))
+            if e == 1:
+                steps += [(quantize_g, 2), (act, 3)]
+            if e == 3:
+                steps.append((quantize_g, 3))
+            if e + 2 < E:
+                steps.append((first_product, e + 2))
+            if e in (1, 3):
+                steps += [(scatter, e // 2, k) for k in range(KT)]
+        for step in steps:
+            load()
+            step[0](*step[1:])
+        for k in range(KT):
+            for pair in (2, 3):
+                scatter(pair, k)
+            nc.sync.dma_start(out[k * P : (k + 1) * P, :], win[k][:])

@@ -26,7 +26,7 @@ J = 4
 PAIR = 2 * C
 KT = K // P
 RAW_BUFS = 9
-ON_VECTOR = {("w2", 1), ("w3", 0), ("w3", 1), ("w3", 3), ("w3", 5), ("w3", 7)}
+ON_VECTOR = {("g", 0), ("g", 3), ("w3", 0), ("w3", 1), ("w3", 2), ("w3", 4), ("w3", 5)}
 
 
 def tile_moe_bdx_glu_silu_kernel(tc, dyT, a1, a3, w2, w1, w3, gate, offs, out):
@@ -55,9 +55,8 @@ def tile_moe_bdx_glu_silu_kernel(tc, dyT, a1, a3, w2, w1, w3, gate, offs, out):
         for k in range(KT):
             nc.gpsimd.memset(win[k][:], 0.0)
 
-        order = [("a1", 0), ("gate", 0), ("a3", 0), ("dy", 0), ("a1", 1), ("dy", 1), ("a3", 1), ("w2", 0), ("dy", 2),
-                 ("a1", 2), ("dy", 3), ("w2", 1), ("a3", 2), ("w1", 0), ("w3", 0), ("w2", 2), ("w1", 1), ("w3", 1),
-                 ("a1", 3), ("a3", 3), ("w2", 3)]
+        order = [("a1", 0), ("a3", 0), ("a1", 1), ("a3", 1), ("gate", 0), ("dy", 0), ("dy", 1), ("a1", 2), ("dy", 2), ("dy", 3),
+                 ("a1", 3), ("a3", 2), ("w2", 0), ("a3", 3), ("w2", 1), ("w3", 0), ("w1", 0), ("w2", 2), ("w3", 1), ("w1", 1), ("w2", 3)]
         for e in range(2, E):
             order += [("w1", e), ("w3", e)]
             if e + 2 < E:
@@ -105,36 +104,57 @@ def tile_moe_bdx_glu_silu_kernel(tc, dyT, a1, a3, w2, w1, w3, gate, offs, out):
         def matmul(dst, lq, ls, m, rq, rs, n, start, stop):
             nc.tensor.matmul_mx(dst, lq[:, m].bitcast(FP8X4), ls[:, m], rq[:, n].bitcast(FP8X4), rs[:, n], start=start, stop=stop)
 
+        acts = {}
+
         def act(q):
             th = work.tile([P, J, PAIR], F32, name="th")
             ng = work.tile([P, J, PAIR], F32, name="ng")
             nc.scalar.activation(th[:], lt[q][:], TANH, scale=0.5)
             nc.scalar.activation(ng[:], lt[q][:], SILU, scale=-1.0)
             nc.scalar.activation(lt[q][:], lt[q][:], SILU)
-            nc.vector.scalar_tensor_tensor(yt[q][:], th[:], 1.0, yt[q][:], ADD, MULT)
-            nc.vector.scalar_tensor_tensor(yt[q][:], ng[:], 1.0, yt[q][:], SUB, MULT)
+            acts[q] = (th, ng)
+
+        def x_factor(q):
+            nc.vector.scalar_tensor_tensor(yt[q][:], acts[q][0][:], 1.0, yt[q][:], ADD, MULT)
+
+        def y_factor(q):
+            nc.vector.scalar_tensor_tensor(yt[q][:], acts[q][1][:], 1.0, yt[q][:], SUB, MULT)
 
         def gather(j):
             window = take("dy", j)
             nc.vector.tensor_tensor(g32[:, j, :], window[:].indirect(offsets[:]), gate_t[:], MULT)
 
-        def quantize_g(q):
+        g_cast = {}
+
+        def cast_g(q):
             cols = slice(q * PAIR, (q + 1) * PAIR)
             gb = work.tile([P, PAIR, J], BF16, name="gb", align_bytes=64)
             cast(("g", q), gb[:].rearrange("p (c i) j -> p c j i", i=4), g32[:, :, cols].rearrange("p j (c i) -> p c j i", i=4))
-            quantize(gq[:, cols], gs[:, cols], gb[:].rearrange("p n j -> p (n j)"))
+            g_cast[q] = gb
+
+        def quantize_g(q):
+            cols = slice(q * PAIR, (q + 1) * PAIR)
+            quantize(gq[:, cols], gs[:, cols], g_cast.pop(q)[:].rearrange("p n j -> p (n j)"))
 
         w2_ready = {}
         da_ready = {}
+        w13_ready = {}
         dx_ready = {}
 
-        def make_w2(e):
+        w2_cast = {}
+        w13_cast = {}
+        da_cast = {}
+
+        def cast_w2(e):
             raw = take("w2", e)
             wb = work.tile([P, J * H], BF16, name="w2b", align_bytes=64)
+            cast(("w2", e), wb[:].rearrange("p (t m j) -> p m j t", t=4, j=J), raw[:].rearrange("p j (m t) -> p m j t", t=4))
+            w2_cast[e] = wb
+
+        def quantize_w2(e):
             wq = work.tile([P, H], U32, name="w2q", align_bytes=64)
             ws = work.tile([P, H], U8, name="w2s", align_bytes=64)
-            cast(("w2", e), wb[:].rearrange("p (t m j) -> p m j t", t=4, j=J), raw[:].rearrange("p j (m t) -> p m j t", t=4))
-            quantize(wq[:], ws[:], wb[:])
+            quantize(wq[:], ws[:], w2_cast.pop(e)[:])
             w2_ready[e] = (wq, ws)
 
         def first_product(e):
@@ -143,24 +163,35 @@ def tile_moe_bdx_glu_silu_kernel(tc, dyT, a1, a3, w2, w1, w3, gate, offs, out):
             for t in range(J):
                 matmul(dh[:, t, :], wq, ws, slice(t * P, (t + 1) * P), gq, gs, slice(e * C, (e + 1) * C), True, True)
             db = work.tile([P, 2, C, J], BF16, name="db", align_bytes=64)
-            dq = more.tile([P, 2 * C], U32, name="dq", align_bytes=64)
-            ds = more.tile([P, 2 * C], U8, name="ds", align_bytes=64)
             sub = slice((e % 2) * C, (e % 2 + 1) * C)
             dhv = dh[:].rearrange("p r n -> p n r")
             nc.vector.scalar_tensor_tensor(db[:, 0, :, :], dhv, -0.5, yt[e // 2][:, :, sub].rearrange("p r n -> p n r"), MULT, MULT)
             nc.vector.tensor_tensor(db[:, 1, :, :], dhv, lt[e // 2][:, :, sub].rearrange("p r n -> p n r"), MULT)
-            quantize(dq[:], ds[:], db[:].rearrange("p a n r -> p (a n r)"))
+            da_cast[e] = db
+
+        def quantize_da(e):
+            dq = more.tile([P, 2 * C], U32, name="dq", align_bytes=64)
+            ds = more.tile([P, 2 * C], U8, name="ds", align_bytes=64)
+            quantize(dq[:], ds[:], da_cast.pop(e)[:].rearrange("p a n r -> p (a n r)"))
             da_ready[e] = (dq, ds)
 
-        def second_product(e):
+        def cast_w13(e):
             wb = work.tile([P, 2 * K, J], BF16, name="wb", align_bytes=64)
-            wq = work.tile([P, 2 * K], U32, name="wq", align_bytes=64)
-            ws = work.tile([P, 2 * K], U8, name="ws", align_bytes=64)
             for a, kind in enumerate(("w1", "w3")):
                 raw = take(kind, e)
                 cast((kind, e), wb[:, a * K : (a + 1) * K, :].rearrange("p (c i) j -> p c j i", i=4), raw[:].rearrange("p j (c i) -> p c j i", i=4))
+            w13_cast[e] = wb
+
+        def quantize_w13(e):
+            wb = w13_cast.pop(e)
+            wq = work.tile([P, 2 * K], U32, name="wq", align_bytes=64)
+            ws = work.tile([P, 2 * K], U8, name="ws", align_bytes=64)
             for lo, hi in ((0, 512), (512, 768)):
                 quantize(wq[:, lo:hi], ws[:, lo:hi], wb[:, lo:hi, :].rearrange("p n j -> p (n j)"))
+            w13_ready[e] = (wq, ws)
+
+        def second_product(e):
+            wq, ws = w13_ready.pop(e)
             dq, ds = da_ready.pop(e)
             dx = psum.tile([P, KT, C], F32, name="dx")
             for k in range(KT):
@@ -176,20 +207,21 @@ def tile_moe_bdx_glu_silu_kernel(tc, dyT, a1, a3, w2, w1, w3, gate, offs, out):
             cols = slice(pair * PAIR // 16, (pair + 1) * PAIR // 16)
             nc.vector.tensor_copy(win[k][:].indirect(offsets[:, cols]), dx_ready[pair][:, k, :])
 
-        steps = [(act, 0), (gather, 0), (gather, 1), (act, 1), (make_w2, 0), (gather, 2), (gather, 3), (act, 2),
-                 (make_w2, 1), (quantize_g, 0), (first_product, 0), (first_product, 1), (quantize_g, 1)]
+        steps = [(act, 0), (x_factor, 0), (act, 1), (x_factor, 1), (y_factor, 0), (y_factor, 1)]
+        steps += [(gather, j) for j in range(J)]
+        steps += [(act, 2), (x_factor, 2), (cast_g, 0), (y_factor, 2), (quantize_g, 0), (cast_g, 1), (act, 3), (cast_w2, 0), (x_factor, 3),
+                  (quantize_g, 1), (cast_w2, 1), (quantize_w2, 0), (cast_g, 2), (y_factor, 3), (cast_g, 3), (quantize_w2, 1), (quantize_g, 2), (quantize_g, 3),
+                  (first_product, 0), (first_product, 1)]
         for e in range(E):
+            if 1 <= e and e + 1 < E:
+                steps += [(quantize_w2, e + 1), (first_product, e + 1)]
+            steps += [(cast_w13, e), (quantize_w13, e)]
+            if e in (2, 4):
+                steps += [(scatter, e // 2 - 1, k) for k in range(KT)]
+            steps += [(quantize_da, x) for x in ((0, 1) if e == 0 else (e + 1,)) if x < E]
             steps.append((second_product, e))
             if e + 2 < E:
-                steps.append((make_w2, e + 2))
-            if e == 1:
-                steps += [(quantize_g, 2), (act, 3)]
-            if e == 3:
-                steps.append((quantize_g, 3))
-            if e + 2 < E:
-                steps.append((first_product, e + 2))
-            if e in (1, 3):
-                steps += [(scatter, e // 2, k) for k in range(KT)]
+                steps.append((cast_w2, e + 2))
         for step in steps:
             load()
             step[0](*step[1:])

@@ -16,6 +16,7 @@ ADD = mybir.AluOpType.add
 SUB = mybir.AluOpType.subtract
 MULT = mybir.AluOpType.mult
 SILU = mybir.ActivationFunctionType.Silu
+COPY = mybir.ActivationFunctionType.Copy
 TANH = mybir.ActivationFunctionType.Tanh
 
 FLOPS = 2 * S * H * N + 2 * 2 * S * H * K
@@ -25,17 +26,15 @@ P = 128
 J = 4
 PAIR = 2 * C
 KT = K // P
-RAW_BUFS = 9
-ON_VECTOR = {("g", 0), ("g", 3), ("w3", 0), ("w3", 1), ("w3", 2), ("w3", 4), ("w3", 5)}
+RAW_BUFS = 4
+ON_VECTOR = {("w1", 5), ("w3", 2), ("g", 0), ("w3", 1), ("w3", 0), ("g", 2), ("g", 1), ("w3", 4), ("g", 3)}
 
 
 def tile_moe_bdx_glu_silu_kernel(tc, dyT, a1, a3, w2, w1, w3, gate, offs, out):
     nc = tc.nc
     with ExitStack() as ctx:
         keep = ctx.enter_context(tc.tile_pool(name="keep", bufs=1))
-        raws = ctx.enter_context(tc.tile_pool(name="raws", bufs=RAW_BUFS))
         work = ctx.enter_context(tc.tile_pool(name="work", bufs=2))
-        more = ctx.enter_context(tc.tile_pool(name="more", bufs=4))
         psum = ctx.enter_context(tc.psum_pool(name="psum", bufs=4))
 
         offsets = keep.tile([P, S // 16], U16, name="offsets")
@@ -55,12 +54,15 @@ def tile_moe_bdx_glu_silu_kernel(tc, dyT, a1, a3, w2, w1, w3, gate, offs, out):
         for k in range(KT):
             nc.gpsimd.memset(win[k][:], 0.0)
 
-        order = [("a1", 0), ("a3", 0), ("a1", 1), ("a3", 1), ("gate", 0), ("dy", 0), ("dy", 1), ("a1", 2), ("dy", 2), ("dy", 3),
-                 ("a1", 3), ("a3", 2), ("w2", 0), ("a3", 3), ("w2", 1), ("w3", 0), ("w1", 0), ("w2", 2), ("w3", 1), ("w1", 1), ("w2", 3)]
-        for e in range(2, E):
-            order += [("w1", e), ("w3", e)]
-            if e + 2 < E:
-                order.append(("w2", e + 2))
+        head = [("gate", 0), ("dy", 3), ("dy", 2), ("dy", 1), ("a1", 0), ("dy", 0), ("w2", 0)]
+        later = [("w1", 0, 2), ("w2", 0, 1), ("a3", 0, 1), ("w3", 1, 2), ("w1", 1, 2), ("w2", 1, 0), ("w3", 0, 1), ("a1", 0, 0)]
+        order = list(head)
+        for s in range(4 + max(x[2] for x in later)):
+            for kind, odd, lag in later:
+                q = s - lag
+                job = (kind, q) if kind in ("a1", "a3") else (kind, 2 * q + odd)
+                if 0 <= q < 4 and job not in order:
+                    order.append(job)
         source = {
             "a1": lambda q: a1.rearrange("(p r) n -> p r n", r=J)[:, :, q * PAIR : (q + 1) * PAIR],
             "a3": lambda q: a3.rearrange("(p r) n -> p r n", r=J)[:, :, q * PAIR : (q + 1) * PAIR],
@@ -73,8 +75,15 @@ def tile_moe_bdx_glu_silu_kernel(tc, dyT, a1, a3, w2, w1, w3, gate, offs, out):
         ringed = {}
         pending = list(order)
 
+        ring = []
+
+        def ring_free(job):
+            if job[0] in ("a1", "a3", "gate") or len(ring) < RAW_BUFS:
+                return True
+            return ring[len(ring) - RAW_BUFS] not in ringed
+
         def load():
-            while pending and len(ringed) < RAW_BUFS:
+            while pending and ring_free(pending[0]):
                 kind, x = pending[0]
                 pending.remove(pending[0])
                 if kind == "a1":
@@ -85,8 +94,9 @@ def tile_moe_bdx_glu_silu_kernel(tc, dyT, a1, a3, w2, w1, w3, gate, offs, out):
                     dst = gate_t
                 else:
                     shape = {"dy": [P, T], "w2": [P, J, H], "w1": [P, J, K], "w3": [P, J, K]}[kind]
-                    dst = raws.tile(shape, F32, name="raw", tag="raw")
+                    dst = work.tile(shape, F32, name="raw", tag="raw", bufs=4)
                     ringed[(kind, x)] = dst
+                    ring.append((kind, x))
                 nc.sync.dma_start(dst[:], source[kind](x))
 
         def take(kind, x):
@@ -96,7 +106,7 @@ def tile_moe_bdx_glu_silu_kernel(tc, dyT, a1, a3, w2, w1, w3, gate, offs, out):
             if job in ON_VECTOR:
                 nc.vector.tensor_copy(dst, src)
             else:
-                nc.scalar.copy(dst, src)
+                nc.scalar.activation(dst, src, COPY)
 
         def quantize(codes, scales, grouped):
             nc.vector.quantize_mx(codes.bitcast(FP8X4), scales, grouped)
@@ -107,8 +117,8 @@ def tile_moe_bdx_glu_silu_kernel(tc, dyT, a1, a3, w2, w1, w3, gate, offs, out):
         acts = {}
 
         def act(q):
-            th = work.tile([P, J, PAIR], F32, name="th")
-            ng = work.tile([P, J, PAIR], F32, name="ng")
+            th = work.tile([P, J, PAIR], F32, name="th", bufs=2)
+            ng = work.tile([P, J, PAIR], F32, name="ng", bufs=5)
             nc.scalar.activation(th[:], lt[q][:], TANH, scale=0.5)
             nc.scalar.activation(ng[:], lt[q][:], SILU, scale=-1.0)
             nc.scalar.activation(lt[q][:], lt[q][:], SILU)
@@ -128,7 +138,7 @@ def tile_moe_bdx_glu_silu_kernel(tc, dyT, a1, a3, w2, w1, w3, gate, offs, out):
 
         def cast_g(q):
             cols = slice(q * PAIR, (q + 1) * PAIR)
-            gb = work.tile([P, PAIR, J], BF16, name="gb", align_bytes=64)
+            gb = work.tile([P, PAIR, J], BF16, name="gb", bufs=6, align_bytes=64)
             cast(("g", q), gb[:].rearrange("p (c i) j -> p c j i", i=4), g32[:, :, cols].rearrange("p j (c i) -> p c j i", i=4))
             g_cast[q] = gb
 
@@ -140,6 +150,7 @@ def tile_moe_bdx_glu_silu_kernel(tc, dyT, a1, a3, w2, w1, w3, gate, offs, out):
         da_ready = {}
         w13_ready = {}
         dx_ready = {}
+        dx_bank = {}
 
         w2_cast = {}
         w13_cast = {}
@@ -147,36 +158,41 @@ def tile_moe_bdx_glu_silu_kernel(tc, dyT, a1, a3, w2, w1, w3, gate, offs, out):
 
         def cast_w2(e):
             raw = take("w2", e)
-            wb = work.tile([P, J * H], BF16, name="w2b", align_bytes=64)
+            wb = work.tile([P, J * H], BF16, name="w2b", bufs=5, align_bytes=64)
             cast(("w2", e), wb[:].rearrange("p (t m j) -> p m j t", t=4, j=J), raw[:].rearrange("p j (m t) -> p m j t", t=4))
             w2_cast[e] = wb
 
         def quantize_w2(e):
-            wq = work.tile([P, H], U32, name="w2q", align_bytes=64)
-            ws = work.tile([P, H], U8, name="w2s", align_bytes=64)
+            wq = work.tile([P, H], U32, name="w2q", bufs=4, align_bytes=64)
+            ws = work.tile([P, H], U8, name="w2s", bufs=4, align_bytes=64)
             quantize(wq[:], ws[:], w2_cast.pop(e)[:])
             w2_ready[e] = (wq, ws)
 
         def first_product(e):
             wq, ws = w2_ready.pop(e)
-            dh = psum.tile([P, J, C], F32, name="dh")
+            dh = psum.tile([P, J, C], F32, name="dh", bufs=2)
             for t in range(J):
                 matmul(dh[:, t, :], wq, ws, slice(t * P, (t + 1) * P), gq, gs, slice(e * C, (e + 1) * C), True, True)
-            db = work.tile([P, 2, C, J], BF16, name="db", align_bytes=64)
+            db = work.tile([P, 2, C, J], BF16, name="db", bufs=2, align_bytes=64)
             sub = slice((e % 2) * C, (e % 2 + 1) * C)
             dhv = dh[:].rearrange("p r n -> p n r")
             nc.vector.scalar_tensor_tensor(db[:, 0, :, :], dhv, -0.5, yt[e // 2][:, :, sub].rearrange("p r n -> p n r"), MULT, MULT)
-            nc.vector.tensor_tensor(db[:, 1, :, :], dhv, lt[e // 2][:, :, sub].rearrange("p r n -> p n r"), MULT)
+            nc.vector.tensor_tensor(
+                db[:, 1, :, :].rearrange("p (c i) r -> p c r i", i=4),
+                dh[:].rearrange("p r (c i) -> p c r i", i=4),
+                lt[e // 2][:, :, sub].rearrange("p r (c i) -> p c r i", i=4),
+                MULT,
+            )
             da_cast[e] = db
 
         def quantize_da(e):
-            dq = more.tile([P, 2 * C], U32, name="dq", align_bytes=64)
-            ds = more.tile([P, 2 * C], U8, name="ds", align_bytes=64)
+            dq = work.tile([P, 2 * C], U32, name="dq", bufs=4, align_bytes=64)
+            ds = work.tile([P, 2 * C], U8, name="ds", bufs=4, align_bytes=64)
             quantize(dq[:], ds[:], da_cast.pop(e)[:].rearrange("p a n r -> p (a n r)"))
             da_ready[e] = (dq, ds)
 
         def cast_w13(e):
-            wb = work.tile([P, 2 * K, J], BF16, name="wb", align_bytes=64)
+            wb = work.tile([P, 2 * K, J], BF16, name="wb", bufs=2, align_bytes=64)
             for a, kind in enumerate(("w1", "w3")):
                 raw = take(kind, e)
                 cast((kind, e), wb[:, a * K : (a + 1) * K, :].rearrange("p (c i) j -> p c j i", i=4), raw[:].rearrange("p j (c i) -> p c j i", i=4))
@@ -184,8 +200,8 @@ def tile_moe_bdx_glu_silu_kernel(tc, dyT, a1, a3, w2, w1, w3, gate, offs, out):
 
         def quantize_w13(e):
             wb = w13_cast.pop(e)
-            wq = work.tile([P, 2 * K], U32, name="wq", align_bytes=64)
-            ws = work.tile([P, 2 * K], U8, name="ws", align_bytes=64)
+            wq = work.tile([P, 2 * K], U32, name="wq", bufs=2, align_bytes=64)
+            ws = work.tile([P, 2 * K], U8, name="ws", bufs=2, align_bytes=64)
             for lo, hi in ((0, 512), (512, 768)):
                 quantize(wq[:, lo:hi], ws[:, lo:hi], wb[:, lo:hi, :].rearrange("p n j -> p (n j)"))
             w13_ready[e] = (wq, ws)
@@ -193,39 +209,44 @@ def tile_moe_bdx_glu_silu_kernel(tc, dyT, a1, a3, w2, w1, w3, gate, offs, out):
         def second_product(e):
             wq, ws = w13_ready.pop(e)
             dq, ds = da_ready.pop(e)
-            dx = psum.tile([P, KT, C], F32, name="dx")
+            dx = psum.tile([P, KT, C], F32, name="dx", bufs=5)
             for k in range(KT):
                 for a in range(2):
                     m = slice(a * K + k * P, a * K + (k + 1) * P)
                     matmul(dx[:, k, :], wq, ws, m, dq, ds, slice(a * C, (a + 1) * C), a == 0, a == 1)
-            if e % 2 == 0:
-                dxs = more.tile([P, KT, PAIR], F32, name="dxs")
+            dx_bank[e] = dx
+
+        def copy_out(e):
+            if e // 2 not in dx_ready:
+                dxs = work.tile([P, KT, PAIR], F32, name="dxs", bufs=3)
                 dx_ready[e // 2] = dxs
-            nc.scalar.copy(dx_ready[e // 2][:, :, (e % 2) * C : (e % 2 + 1) * C], dx[:])
+            half = dx_ready[e // 2][:, :, (e % 2) * C : (e % 2 + 1) * C]
+            if ("ev", e) in ON_VECTOR:
+                nc.vector.tensor_copy(half, dx_bank.pop(e)[:])
+            else:
+                nc.scalar.copy(half, dx_bank.pop(e)[:])
+
+        def store(k):
+            nc.sync.dma_start(out[k * P : (k + 1) * P, :], win[k][:])
 
         def scatter(pair, k):
             cols = slice(pair * PAIR // 16, (pair + 1) * PAIR // 16)
             nc.vector.tensor_copy(win[k][:].indirect(offsets[:, cols]), dx_ready[pair][:, k, :])
 
-        steps = [(act, 0), (x_factor, 0), (act, 1), (x_factor, 1), (y_factor, 0), (y_factor, 1)]
-        steps += [(gather, j) for j in range(J)]
-        steps += [(act, 2), (x_factor, 2), (cast_g, 0), (y_factor, 2), (quantize_g, 0), (cast_g, 1), (act, 3), (cast_w2, 0), (x_factor, 3),
-                  (quantize_g, 1), (cast_w2, 1), (quantize_w2, 0), (cast_g, 2), (y_factor, 3), (cast_g, 3), (quantize_w2, 1), (quantize_g, 2), (quantize_g, 3),
-                  (first_product, 0), (first_product, 1)]
-        for e in range(E):
-            if 1 <= e and e + 1 < E:
-                steps += [(quantize_w2, e + 1), (first_product, e + 1)]
-            steps += [(cast_w13, e), (quantize_w13, e)]
-            if e in (2, 4):
-                steps += [(scatter, e // 2 - 1, k) for k in range(KT)]
-            steps += [(quantize_da, x) for x in ((0, 1) if e == 0 else (e + 1,)) if x < E]
-            steps.append((second_product, e))
-            if e + 2 < E:
-                steps.append((cast_w2, e + 2))
+        steps = [(gather, 2), (gather, 1), (act, 0), (gather, 0), (gather, 3), (act, 1), (cast_w2, 0), (cast_g, 2), (cast_g, 3), (cast_g, 0), (cast_g, 1), (quantize_g, 3), (quantize_g, 1), (quantize_g, 2), (cast_w2, 1), (quantize_g, 0)]
+        later_steps = [(act, 0, 0), (quantize_da, 1, 2), (copy_out, 1, 3), (y_factor, 0, 1), (cast_w2, 1, 0), (quantize_w13, 1, 2), (quantize_w2, 1, 0), (quantize_da, 0, 2), (first_product, 1, 1), (cast_w13, 1, 1), (copy_out, 0, 3), (second_product, 0, 2), (quantize_w13, 0, 1), (cast_w2, 0, 0), (quantize_w2, 0, 0), (cast_w13, 0, 0), (x_factor, 0, 0), (first_product, 0, 1), (scatter, 0, 3), (scatter, 1, 3), (second_product, 1, 2), (scatter, 2, 3)]
+        for s in range(4 + max(x[2] for x in later_steps)):
+            for what, odd, lag in later_steps:
+                q = s - lag
+                if what in (act, x_factor, y_factor):
+                    step = (what, q)
+                elif what is scatter:
+                    step = (what, q, odd)
+                else:
+                    step = (what, 2 * q + odd)
+                if 0 <= q < 4 and step not in steps:
+                    steps.append(step)
+        steps += [(store, k) for k in range(KT)]
         for step in steps:
             load()
             step[0](*step[1:])
-        for k in range(KT):
-            for pair in (2, 3):
-                scatter(pair, k)
-            nc.sync.dma_start(out[k * P : (k + 1) * P, :], win[k][:])

@@ -6,6 +6,15 @@ N, T, H, K = 512, 2048, 512, 384
 E, C = 8, 128
 S = E * C
 
+P = 128
+J = 4
+PAIR = 2 * C
+PAIRS = E // 2
+KT = K // P
+
+FLOPS = 2 * S * H * N + 2 * 2 * S * H * K
+BYTES = 4 * (N * T + 2 * H * S + E * N * H + 2 * E * H * K + S + K * T) + 2 * 8 * S
+
 F32 = mybir.dt.float32
 BF16 = mybir.dt.bfloat16
 U32 = mybir.dt.uint32
@@ -15,19 +24,29 @@ FP8X4 = mybir.dt.float8_e4m3fn_x4
 ADD = mybir.AluOpType.add
 SUB = mybir.AluOpType.subtract
 MULT = mybir.AluOpType.mult
-SILU = mybir.ActivationFunctionType.Silu
 COPY = mybir.ActivationFunctionType.Copy
+SILU = mybir.ActivationFunctionType.Silu
 TANH = mybir.ActivationFunctionType.Tanh
 
-FLOPS = 2 * S * H * N + 2 * 2 * S * H * K
-BYTES = 4 * (N * T + 2 * H * S + E * N * H + 2 * E * H * K + S + K * T) + 2 * S
+RING = 5
 
-P = 128
-J = 4
-PAIR = 2 * C
-KT = K // P
-RAW_BUFS = 4
-ON_VECTOR = {("w1", 5), ("w3", 2), ("g", 0), ("w3", 1), ("w3", 0), ("g", 2), ("g", 1), ("w3", 4), ("g", 3)}
+ON_VECTOR = {("w1" if e % 2 else "w3", e) for e in range(5)}
+
+FIRST_LOADS = [("a1", 1), ("dyT", 0), ("gate", 0), ("dyT", 1), ("dyT", 2), ("dyT", 3), ("a1", 0), ("a3", 1), ("w2", 0)]
+PAIR_LOADS = [
+    ("w2", 0, 1),
+    ("w3", 0, 2),
+    ("w2", 1, 1),
+    ("a1", 0, 1),
+    ("w3", 1, 2),
+    ("w1", 1, 2),
+    ("a3", 0, 1),
+    ("w1", 0, 1),
+]
+
+
+def row_tiles(e):
+    return [(0, 2), (2, 3)] if e // 2 == PAIRS - 1 else [(0, KT)]
 
 
 def tile_moe_bdx_glu_silu_kernel(tc, dyT, a1, a3, w2, w1, w3, gate, offs, out):
@@ -35,7 +54,7 @@ def tile_moe_bdx_glu_silu_kernel(tc, dyT, a1, a3, w2, w1, w3, gate, offs, out):
     with ExitStack() as ctx:
         keep = ctx.enter_context(tc.tile_pool(name="keep", bufs=1))
         work = ctx.enter_context(tc.tile_pool(name="work", bufs=2))
-        psum = ctx.enter_context(tc.psum_pool(name="psum", bufs=4))
+        psum = ctx.enter_context(tc.psum_pool(name="psum", bufs=2))
 
         offsets = keep.tile([P, S // 16], U16, name="offsets")
         nc.sync.dma_start(offsets[:], offs)
@@ -44,209 +63,252 @@ def tile_moe_bdx_glu_silu_kernel(tc, dyT, a1, a3, w2, w1, w3, gate, offs, out):
         nc.vector.memset(warm[:], 0.0)
         nc.scalar.activation(warm[:], warm[:], SILU)
 
-        gate_t = keep.tile([P, S], F32, name="gate_t")
-        lt = [keep.tile([P, J, PAIR], F32, name=f"l{q}") for q in range(4)]
-        yt = [keep.tile([P, J, PAIR], F32, name=f"y{q}") for q in range(4)]
-        win = [keep.tile([P, T], F32, name=f"win{k}") for k in range(KT)]
-        g32 = keep.tile([P, J, S], F32, name="g32")
-        gq = keep.tile([P, S], U32, name="gq", align_bytes=64)
-        gs = keep.tile([P, S], U8, name="gs", align_bytes=64)
+        results = [keep.tile([P, T], F32, name=f"result{k}") for k in range(KT)]
         for k in range(KT):
-            nc.gpsimd.memset(win[k][:], 0.0)
+            nc.gpsimd.memset(results[k][:], 0.0)
 
-        head = [("gate", 0), ("dy", 3), ("dy", 2), ("dy", 1), ("a1", 0), ("dy", 0), ("w2", 0)]
-        later = [("w1", 0, 2), ("w2", 0, 1), ("a3", 0, 1), ("w3", 1, 2), ("w1", 1, 2), ("w2", 1, 0), ("w3", 0, 1), ("a1", 0, 0)]
-        order = list(head)
-        for s in range(4 + max(x[2] for x in later)):
-            for kind, odd, lag in later:
+        gate_rows = keep.tile([P, S], F32, name="gate_rows")
+        silu_a1 = [keep.tile([P, J, PAIR], F32, name=f"silu_a1_{q}") for q in range(PAIRS)]
+        factor = [keep.tile([P, J, PAIR], F32, name=f"factor_{q}") for q in range(PAIRS)]
+        g = keep.tile([P, J, S], F32, name="g")
+        g_grouped = keep.tile([P, S, J], BF16, name="g_grouped", align_bytes=64)
+        g_codes = keep.tile([P, S], U32, name="g_codes", align_bytes=64)
+        g_scales = keep.tile([P, S], U8, name="g_scales", align_bytes=64)
+
+        loads = list(FIRST_LOADS)
+        for s in range(PAIRS + max(lag for name, member, lag in PAIR_LOADS)):
+            for name, member, lag in PAIR_LOADS:
                 q = s - lag
-                job = (kind, q) if kind in ("a1", "a3") else (kind, 2 * q + odd)
-                if 0 <= q < 4 and job not in order:
-                    order.append(job)
-        source = {
-            "a1": lambda q: a1.rearrange("(p r) n -> p r n", r=J)[:, :, q * PAIR : (q + 1) * PAIR],
-            "a3": lambda q: a3.rearrange("(p r) n -> p r n", r=J)[:, :, q * PAIR : (q + 1) * PAIR],
-            "gate": lambda q: gate[0:P, :],
-            "dy": lambda j: dyT.rearrange("(p j) t -> p j t", j=J)[:, j, :],
-            "w2": lambda e: w2[e].rearrange("(p j) i -> p j i", j=J),
-            "w1": lambda e: w1[e].rearrange("(p j) k -> p j k", j=J),
-            "w3": lambda e: w3[e].rearrange("(p j) k -> p j k", j=J),
-        }
-        ringed = {}
-        pending = list(order)
-
+                load = (name, q) if name in ("a1", "a3") else (name, 2 * q + member)
+                if 0 <= q < PAIRS and load not in loads:
+                    loads.append(load)
+        held = {}
         ring = []
 
-        def ring_free(job):
-            if job[0] in ("a1", "a3", "gate") or len(ring) < RAW_BUFS:
-                return True
-            return ring[len(ring) - RAW_BUFS] not in ringed
+        def pair_columns(x, q):
+            return x.rearrange("(p r) c -> p r c", r=J)[:, :, q * PAIR : (q + 1) * PAIR]
 
-        def load():
-            while pending and ring_free(pending[0]):
-                kind, x = pending[0]
-                pending.remove(pending[0])
-                if kind == "a1":
-                    dst = lt[x]
-                elif kind == "a3":
-                    dst = yt[x]
-                elif kind == "gate":
-                    dst = gate_t
+        def load_ahead():
+            while loads:
+                name, x = loads[0]
+                if name == "a1":
+                    tile, source = silu_a1[x], pair_columns(a1, x)
+                elif name == "a3":
+                    tile, source = factor[x], pair_columns(a3, x)
+                elif name == "gate":
+                    tile, source = gate_rows, gate[0:P, :]
                 else:
-                    shape = {"dy": [P, T], "w2": [P, J, H], "w1": [P, J, K], "w3": [P, J, K]}[kind]
-                    dst = work.tile(shape, F32, name="raw", tag="raw", bufs=4)
-                    ringed[(kind, x)] = dst
-                    ring.append((kind, x))
-                nc.sync.dma_start(dst[:], source[kind](x))
+                    if len(ring) >= RING and ring[len(ring) - RING] in held:
+                        return
+                    if name == "dyT":
+                        raw = work.tile([P, T], F32, name="raw", bufs=RING)
+                        source = dyT.rearrange("(p j) t -> p j t", j=J)[:, x, :]
+                    else:
+                        weight, width = {"w2": (w2, H), "w1": (w1, K), "w3": (w3, K)}[name]
+                        raw = work.tile([P, J, width], F32, name="raw", bufs=RING)
+                        source = weight[x].rearrange("(p j) i -> p j i", j=J)
+                    tile = raw
+                    held[(name, x)] = raw
+                    ring.append((name, x))
+                nc.sync.dma_start(tile[:], source)
+                loads.remove((name, x))
 
-        def take(kind, x):
-            return ringed.pop((kind, x))
-
-        def cast(job, dst, src):
-            if job in ON_VECTOR:
-                nc.vector.tensor_copy(dst, src)
+        def round_into(on_vector, grouped, rows):
+            if on_vector:
+                nc.vector.tensor_copy(grouped, rows)
             else:
-                nc.scalar.activation(dst, src, COPY)
+                nc.scalar.activation(grouped, rows, COPY)
+
+        def by_fours(grouped, rows):
+            return (
+                grouped.rearrange("p (c i) j -> p c j i", i=4),
+                rows.rearrange("p j (c i) -> p c j i", i=4),
+            )
 
         def quantize(codes, scales, grouped):
             nc.vector.quantize_mx(codes.bitcast(FP8X4), scales, grouped)
 
-        def matmul(dst, lq, ls, m, rq, rs, n, start, stop):
-            nc.tensor.matmul_mx(dst, lq[:, m].bitcast(FP8X4), ls[:, m], rq[:, n].bitcast(FP8X4), rs[:, n], start=start, stop=stop)
+        def multiply(bank, weights, m, moving, n, start, stop):
+            nc.tensor.matmul_mx(
+                bank,
+                weights[0][:, m].bitcast(FP8X4),
+                weights[1][:, m],
+                moving[0][:, n].bitcast(FP8X4),
+                moving[1][:, n],
+                start=start,
+                stop=stop,
+            )
 
-        acts = {}
+        tanh_a1, silu_minus_a1 = {}, {}
+        w2_grouped, w2_packed = {}, {}
+        da_grouped, da_packed = {}, {}
+        w13_grouped, w13_packed = {}, {}
+        dx_banks, dx_pairs = {}, {}
 
-        def act(q):
-            th = work.tile([P, J, PAIR], F32, name="th", bufs=2)
-            ng = work.tile([P, J, PAIR], F32, name="ng", bufs=5)
-            nc.scalar.activation(th[:], lt[q][:], TANH, scale=0.5)
-            nc.scalar.activation(ng[:], lt[q][:], SILU, scale=-1.0)
-            nc.scalar.activation(lt[q][:], lt[q][:], SILU)
-            acts[q] = (th, ng)
+        def activate(q):
+            tanh_half = work.tile([P, J, PAIR], F32, name="tanh_half")
+            minus = work.tile([P, J, PAIR], F32, name="minus")
+            nc.scalar.activation(tanh_half[:], silu_a1[q][:], TANH, scale=0.5)
+            nc.scalar.activation(minus[:], silu_a1[q][:], SILU, scale=-1.0)
+            nc.scalar.activation(silu_a1[q][:], silu_a1[q][:], SILU)
+            tanh_a1[q], silu_minus_a1[q] = tanh_half, minus
 
-        def x_factor(q):
-            nc.vector.scalar_tensor_tensor(yt[q][:], acts[q][0][:], 1.0, yt[q][:], ADD, MULT)
+        def times_sigmoid(q):
+            nc.vector.scalar_tensor_tensor(factor[q][:], tanh_a1.pop(q)[:], 1.0, factor[q][:], ADD, MULT)
 
-        def y_factor(q):
-            nc.vector.scalar_tensor_tensor(yt[q][:], acts[q][1][:], 1.0, yt[q][:], SUB, MULT)
+        def times_rest(q):
+            nc.vector.scalar_tensor_tensor(factor[q][:], silu_minus_a1.pop(q)[:], 1.0, factor[q][:], SUB, MULT)
 
         def gather(j):
-            window = take("dy", j)
-            nc.vector.tensor_tensor(g32[:, j, :], window[:].indirect(offsets[:]), gate_t[:], MULT)
+            rows = held.pop(("dyT", j))
+            nc.vector.tensor_tensor(g[:, j, :], rows[:].indirect(offsets[:]), gate_rows[:], MULT)
 
-        g_cast = {}
+        def round_g():
+            round_into(True, *by_fours(g_grouped[:], g[:]))
 
-        def cast_g(q):
-            cols = slice(q * PAIR, (q + 1) * PAIR)
-            gb = work.tile([P, PAIR, J], BF16, name="gb", bufs=6, align_bytes=64)
-            cast(("g", q), gb[:].rearrange("p (c i) j -> p c j i", i=4), g32[:, :, cols].rearrange("p j (c i) -> p c j i", i=4))
-            g_cast[q] = gb
+        def quantize_g():
+            quantize(g_codes[:], g_scales[:], g_grouped[:].rearrange("p c j -> p (c j)"))
 
-        def quantize_g(q):
-            cols = slice(q * PAIR, (q + 1) * PAIR)
-            quantize(gq[:, cols], gs[:, cols], g_cast.pop(q)[:].rearrange("p n j -> p (n j)"))
-
-        w2_ready = {}
-        da_ready = {}
-        w13_ready = {}
-        dx_ready = {}
-        dx_bank = {}
-
-        w2_cast = {}
-        w13_cast = {}
-        da_cast = {}
-
-        def cast_w2(e):
-            raw = take("w2", e)
-            wb = work.tile([P, J * H], BF16, name="w2b", bufs=5, align_bytes=64)
-            cast(("w2", e), wb[:].rearrange("p (t m j) -> p m j t", t=4, j=J), raw[:].rearrange("p j (m t) -> p m j t", t=4))
-            w2_cast[e] = wb
+        def round_w2(e):
+            raw = held.pop(("w2", e))
+            grouped = work.tile([P, H * J], BF16, name="w2_words", bufs=3, align_bytes=64)
+            round_into(
+                False,
+                grouped[:].rearrange("p (t m j) -> p m j t", t=J, j=J),
+                raw[:].rearrange("p j (m t) -> p m j t", t=J),
+            )
+            w2_grouped[e] = grouped
 
         def quantize_w2(e):
-            wq = work.tile([P, H], U32, name="w2q", bufs=4, align_bytes=64)
-            ws = work.tile([P, H], U8, name="w2s", bufs=4, align_bytes=64)
-            quantize(wq[:], ws[:], w2_cast.pop(e)[:])
-            w2_ready[e] = (wq, ws)
+            codes = work.tile([P, H], U32, name="w2_codes", bufs=4, align_bytes=64)
+            scales = work.tile([P, H], U8, name="w2_scales", bufs=4, align_bytes=64)
+            quantize(codes[:], scales[:], w2_grouped.pop(e)[:])
+            w2_packed[e] = (codes, scales)
 
         def first_product(e):
-            wq, ws = w2_ready.pop(e)
-            dh = psum.tile([P, J, C], F32, name="dh", bufs=2)
+            packed = w2_packed.pop(e)
+            dh = psum.tile([P, J, C], F32, name="dh")
             for t in range(J):
-                matmul(dh[:, t, :], wq, ws, slice(t * P, (t + 1) * P), gq, gs, slice(e * C, (e + 1) * C), True, True)
-            db = work.tile([P, 2, C, J], BF16, name="db", bufs=2, align_bytes=64)
-            sub = slice((e % 2) * C, (e % 2 + 1) * C)
-            dhv = dh[:].rearrange("p r n -> p n r")
-            nc.vector.scalar_tensor_tensor(db[:, 0, :, :], dhv, -0.5, yt[e // 2][:, :, sub].rearrange("p r n -> p n r"), MULT, MULT)
-            nc.vector.tensor_tensor(
-                db[:, 1, :, :].rearrange("p (c i) r -> p c r i", i=4),
-                dh[:].rearrange("p r (c i) -> p c r i", i=4),
-                lt[e // 2][:, :, sub].rearrange("p r (c i) -> p c r i", i=4),
+                multiply(dh[:, t, :], packed, slice(t * P, (t + 1) * P), (g_codes, g_scales), slice(e * C, (e + 1) * C), True, True)
+            grouped = work.tile([P, 2, C, J], BF16, name="da_words", align_bytes=64)
+            q, half = e // 2, slice((e % 2) * C, (e % 2 + 1) * C)
+            nc.vector.scalar_tensor_tensor(
+                grouped[:, 0, :, :],
+                dh[:].rearrange("p r c -> p c r"),
+                -0.5,
+                factor[q][:, :, half].rearrange("p r c -> p c r"),
+                MULT,
                 MULT,
             )
-            da_cast[e] = db
+            words, sums = by_fours(grouped[:, 1, :, :], dh[:])
+            nc.vector.tensor_tensor(words, sums, silu_a1[q][:, :, half].rearrange("p r (c i) -> p c r i", i=4), MULT)
+            da_grouped[e] = grouped
 
         def quantize_da(e):
-            dq = work.tile([P, 2 * C], U32, name="dq", bufs=4, align_bytes=64)
-            ds = work.tile([P, 2 * C], U8, name="ds", bufs=4, align_bytes=64)
-            quantize(dq[:], ds[:], da_cast.pop(e)[:].rearrange("p a n r -> p (a n r)"))
-            da_ready[e] = (dq, ds)
+            codes = work.tile([P, 2 * C], U32, name="da_codes", bufs=3, align_bytes=64)
+            scales = work.tile([P, 2 * C], U8, name="da_scales", bufs=3, align_bytes=64)
+            quantize(codes[:], scales[:], da_grouped.pop(e)[:].rearrange("p a c r -> p (a c r)"))
+            da_packed[e] = (codes, scales)
 
-        def cast_w13(e):
-            wb = work.tile([P, 2 * K, J], BF16, name="wb", bufs=2, align_bytes=64)
-            for a, kind in enumerate(("w1", "w3")):
-                raw = take(kind, e)
-                cast((kind, e), wb[:, a * K : (a + 1) * K, :].rearrange("p (c i) j -> p c j i", i=4), raw[:].rearrange("p j (c i) -> p c j i", i=4))
-            w13_cast[e] = wb
+        def round_w13(e, part=0):
+            first, last = row_tiles(e)[part]
+            if part == 0:
+                grouped = work.tile([P, 2 * K, J], BF16, name="w13_words", align_bytes=64)
+                w13_grouped[e] = grouped
+            width = (last - first) * P
+            for i, name in enumerate(("w1", "w3")):
+                raw = held[(name, e)]
+                if last == KT:
+                    held.pop((name, e))
+                at = 2 * P * first + i * width
+                round_into(
+                    (name, e) in ON_VECTOR,
+                    *by_fours(w13_grouped[e][:, at : at + width, :], raw[:, :, first * P : last * P]),
+                )
 
-        def quantize_w13(e):
-            wb = w13_cast.pop(e)
-            wq = work.tile([P, 2 * K], U32, name="wq", bufs=2, align_bytes=64)
-            ws = work.tile([P, 2 * K], U8, name="ws", bufs=2, align_bytes=64)
-            for lo, hi in ((0, 512), (512, 768)):
-                quantize(wq[:, lo:hi], ws[:, lo:hi], wb[:, lo:hi, :].rearrange("p n j -> p (n j)"))
-            w13_ready[e] = (wq, ws)
+        def quantize_w13(e, part=0):
+            first, last = row_tiles(e)[part]
+            if part == 0:
+                codes = work.tile([P, 2 * K], U32, name="w13_codes", align_bytes=64)
+                scales = work.tile([P, 2 * K], U8, name="w13_scales", align_bytes=64)
+                w13_packed[e] = (codes, scales)
+            at, end = 2 * P * first, 2 * P * last
+            while at < end:
+                upto = min(at + 512, end)
+                quantize(
+                    w13_packed[e][0][:, at:upto],
+                    w13_packed[e][1][:, at:upto],
+                    w13_grouped[e][:, at:upto, :].rearrange("p c j -> p (c j)"),
+                )
+                at = upto
 
-        def second_product(e):
-            wq, ws = w13_ready.pop(e)
-            dq, ds = da_ready.pop(e)
-            dx = psum.tile([P, KT, C], F32, name="dx", bufs=5)
-            for k in range(KT):
-                for a in range(2):
-                    m = slice(a * K + k * P, a * K + (k + 1) * P)
-                    matmul(dx[:, k, :], wq, ws, m, dq, ds, slice(a * C, (a + 1) * C), a == 0, a == 1)
-            dx_bank[e] = dx
+        def second_product(e, part=0):
+            first, last = row_tiles(e)[part]
+            dx = psum.tile([P, last - first, C], F32, name="dx", bufs=4)
+            for k in range(first, last):
+                for i in range(2):
+                    at = 2 * P * first + i * (last - first) * P + (k - first) * P
+                    multiply(dx[:, k - first, :], w13_packed[e], slice(at, at + P), da_packed[e], slice(i * C, (i + 1) * C), i == 0, i == 1)
+            dx_banks[(e, part)] = dx
 
-        def copy_out(e):
-            if e // 2 not in dx_ready:
-                dxs = work.tile([P, KT, PAIR], F32, name="dxs", bufs=3)
-                dx_ready[e // 2] = dxs
-            half = dx_ready[e // 2][:, :, (e % 2) * C : (e % 2 + 1) * C]
-            if ("ev", e) in ON_VECTOR:
-                nc.vector.tensor_copy(half, dx_bank.pop(e)[:])
-            else:
-                nc.scalar.copy(half, dx_bank.pop(e)[:])
+        def copy_dx(e, part=0):
+            first, last = row_tiles(e)[part]
+            if e // 2 not in dx_pairs:
+                dx_pair = work.tile([P, KT, PAIR], F32, name="dx_pair")
+                dx_pairs[e // 2] = dx_pair
+            half = slice((e % 2) * C, (e % 2 + 1) * C)
+            nc.scalar.copy(dx_pairs[e // 2][:, first:last, half], dx_banks.pop((e, part))[:])
+
+        def scatter(q, k):
+            columns = slice(q * PAIR // 16, (q + 1) * PAIR // 16)
+            nc.vector.tensor_copy(results[k][:].indirect(offsets[:, columns]), dx_pairs[q][:, k, :])
 
         def store(k):
-            nc.sync.dma_start(out[k * P : (k + 1) * P, :], win[k][:])
+            nc.sync.dma_start(out[k * P : (k + 1) * P, :], results[k][:])
 
-        def scatter(pair, k):
-            cols = slice(pair * PAIR // 16, (pair + 1) * PAIR // 16)
-            nc.vector.tensor_copy(win[k][:].indirect(offsets[:, cols]), dx_ready[pair][:, k, :])
-
-        steps = [(gather, 2), (gather, 1), (act, 0), (gather, 0), (gather, 3), (act, 1), (cast_w2, 0), (cast_g, 2), (cast_g, 3), (cast_g, 0), (cast_g, 1), (quantize_g, 3), (quantize_g, 1), (quantize_g, 2), (cast_w2, 1), (quantize_g, 0)]
-        later_steps = [(act, 0, 0), (quantize_da, 1, 2), (copy_out, 1, 3), (y_factor, 0, 1), (cast_w2, 1, 0), (quantize_w13, 1, 2), (quantize_w2, 1, 0), (quantize_da, 0, 2), (first_product, 1, 1), (cast_w13, 1, 1), (copy_out, 0, 3), (second_product, 0, 2), (quantize_w13, 0, 1), (cast_w2, 0, 0), (quantize_w2, 0, 0), (cast_w13, 0, 0), (x_factor, 0, 0), (first_product, 0, 1), (scatter, 0, 3), (scatter, 1, 3), (second_product, 1, 2), (scatter, 2, 3)]
-        for s in range(4 + max(x[2] for x in later_steps)):
-            for what, odd, lag in later_steps:
+        of_pair = (activate, times_sigmoid, times_rest)
+        pair_steps = [
+            (quantize_da, 0, 2),
+            (round_w2, 0, 0),
+            (round_w13, 0, 1),
+            (activate, 0, 0),
+            (round_w2, 1, 0),
+            (times_sigmoid, 0, 0),
+            (quantize_w13, 1, 2),
+            (quantize_w2, 0, 0),
+            (scatter, 0, 3),
+            (second_product, 0, 2),
+            (quantize_w2, 1, 0),
+            (first_product, 0, 1),
+            (scatter, 1, 3),
+            (copy_dx, 0, 2),
+            (quantize_da, 1, 1),
+            (second_product, 1, 2),
+            (times_rest, 0, 0),
+            (copy_dx, 1, 2),
+            (round_w13, 1, 1),
+            (first_product, 1, 0),
+            (quantize_w13, 0, 1),
+            (scatter, 2, 3),
+        ]
+        steps = [(gather, j) for j in range(J)] + [(round_g,), (quantize_g,)]
+        for s in range(PAIRS + max(lag for function, member, lag in pair_steps)):
+            for function, member, lag in pair_steps:
                 q = s - lag
-                if what in (act, x_factor, y_factor):
-                    step = (what, q)
-                elif what is scatter:
-                    step = (what, q, odd)
+                if not 0 <= q < PAIRS:
+                    continue
+                if function in of_pair:
+                    steps.append((function, q))
+                elif function is scatter:
+                    steps.append((function, q, member))
                 else:
-                    step = (what, 2 * q + odd)
-                if 0 <= q < 4 and step not in steps:
-                    steps.append(step)
+                    steps.append((function, 2 * q + member))
+        late = (scatter, PAIRS - 1, KT - 1)
+        steps.remove(late)
+        for e in (E - 2, E - 1):
+            steps += [(function, e, 1) for function in (round_w13, quantize_w13, second_product, copy_dx)]
+        steps.append(late)
         steps += [(store, k) for k in range(KT)]
         for step in steps:
-            load()
+            load_ahead()
             step[0](*step[1:])

from contextlib import ExitStack

import concourse.mybir as mybir

N, T, H, K = 512, 2048, 512, 384
E, C = 8, 128
S = E * C

P = 128
J = 4
PAIR = 2 * C
PAIRS = E // 2
KT = K // P

FLOPS = 2 * S * H * N + 2 * 2 * S * H * K
BYTES = 4 * (N * T + 2 * H * S + E * N * H + 2 * E * H * K + S + K * T) + 2 * 8 * S

F32 = mybir.dt.float32
BF16 = mybir.dt.bfloat16
U32 = mybir.dt.uint32
U16 = mybir.dt.uint16
U8 = mybir.dt.uint8
FP8X4 = mybir.dt.float8_e4m3fn_x4
ADD = mybir.AluOpType.add
SUB = mybir.AluOpType.subtract
MULT = mybir.AluOpType.mult
COPY = mybir.ActivationFunctionType.Copy
SILU = mybir.ActivationFunctionType.Silu
TANH = mybir.ActivationFunctionType.Tanh

RING = 5

ON_VECTOR = {("w1" if e % 2 else "w3", e) for e in range(5)}

FIRST_LOADS = [("a1", 1), ("dyT", 0), ("gate", 0), ("dyT", 1), ("dyT", 2), ("dyT", 3), ("a1", 0), ("a3", 1), ("w2", 0)]
PAIR_LOADS = [
    ("w2", 0, 1),
    ("w3", 0, 2),
    ("w2", 1, 1),
    ("a1", 0, 1),
    ("w3", 1, 2),
    ("w1", 1, 2),
    ("a3", 0, 1),
    ("w1", 0, 1),
]


def row_tiles(e):
    return [(0, 2), (2, 3)] if e // 2 == PAIRS - 1 else [(0, KT)]


def tile_moe_bdx_glu_silu_kernel(tc, dyT, a1, a3, w2, w1, w3, gate, offs, out):
    nc = tc.nc
    with ExitStack() as ctx:
        keep = ctx.enter_context(tc.tile_pool(name="keep", bufs=1))
        work = ctx.enter_context(tc.tile_pool(name="work", bufs=2))
        psum = ctx.enter_context(tc.psum_pool(name="psum", bufs=2))

        offsets = keep.tile([P, S // 16], U16, name="offsets")
        nc.sync.dma_start(offsets[:], offs)

        warm = keep.tile([P, 1], F32, name="warm")
        nc.vector.memset(warm[:], 0.0)
        nc.scalar.activation(warm[:], warm[:], SILU)

        results = [keep.tile([P, T], F32, name=f"result{k}") for k in range(KT)]
        for k in range(KT):
            nc.gpsimd.memset(results[k][:], 0.0)

        gate_rows = keep.tile([P, S], F32, name="gate_rows")
        silu_a1 = [keep.tile([P, J, PAIR], F32, name=f"silu_a1_{q}") for q in range(PAIRS)]
        factor = [keep.tile([P, J, PAIR], F32, name=f"factor_{q}") for q in range(PAIRS)]
        g = keep.tile([P, J, S], F32, name="g")
        g_grouped = keep.tile([P, S, J], BF16, name="g_grouped", align_bytes=64)
        g_codes = keep.tile([P, S], U32, name="g_codes", align_bytes=64)
        g_scales = keep.tile([P, S], U8, name="g_scales", align_bytes=64)

        loads = list(FIRST_LOADS)
        for s in range(PAIRS + max(lag for name, member, lag in PAIR_LOADS)):
            for name, member, lag in PAIR_LOADS:
                q = s - lag
                load = (name, q) if name in ("a1", "a3") else (name, 2 * q + member)
                if 0 <= q < PAIRS and load not in loads:
                    loads.append(load)
        held = {}
        ring = []

        def pair_columns(x, q):
            return x.rearrange("(p r) c -> p r c", r=J)[:, :, q * PAIR : (q + 1) * PAIR]

        def load_ahead():
            while loads:
                name, x = loads[0]
                if name == "a1":
                    tile, source = silu_a1[x], pair_columns(a1, x)
                elif name == "a3":
                    tile, source = factor[x], pair_columns(a3, x)
                elif name == "gate":
                    tile, source = gate_rows, gate[0:P, :]
                else:
                    if len(ring) >= RING and ring[len(ring) - RING] in held:
                        return
                    if name == "dyT":
                        raw = work.tile([P, T], F32, name="raw", bufs=RING)
                        source = dyT.rearrange("(p j) t -> p j t", j=J)[:, x, :]
                    else:
                        weight, width = {"w2": (w2, H), "w1": (w1, K), "w3": (w3, K)}[name]
                        raw = work.tile([P, J, width], F32, name="raw", bufs=RING)
                        source = weight[x].rearrange("(p j) i -> p j i", j=J)
                    tile = raw
                    held[(name, x)] = raw
                    ring.append((name, x))
                nc.sync.dma_start(tile[:], source)
                loads.remove((name, x))

        def round_into(on_vector, grouped, rows):
            if on_vector:
                nc.vector.tensor_copy(grouped, rows)
            else:
                nc.scalar.activation(grouped, rows, COPY)

        def by_fours(grouped, rows):
            return (
                grouped.rearrange("p (c i) j -> p c j i", i=4),
                rows.rearrange("p j (c i) -> p c j i", i=4),
            )

        def quantize(codes, scales, grouped):
            nc.vector.quantize_mx(codes.bitcast(FP8X4), scales, grouped)

        def multiply(bank, weights, m, moving, n, start, stop):
            nc.tensor.matmul_mx(
                bank,
                weights[0][:, m].bitcast(FP8X4),
                weights[1][:, m],
                moving[0][:, n].bitcast(FP8X4),
                moving[1][:, n],
                start=start,
                stop=stop,
            )

        tanh_a1, silu_minus_a1 = {}, {}
        w2_grouped, w2_packed = {}, {}
        da_grouped, da_packed = {}, {}
        w13_grouped, w13_packed = {}, {}
        dx_banks, dx_pairs = {}, {}

        def activate(q):
            tanh_half = work.tile([P, J, PAIR], F32, name="tanh_half")
            minus = work.tile([P, J, PAIR], F32, name="minus")
            nc.scalar.activation(tanh_half[:], silu_a1[q][:], TANH, scale=0.5)
            nc.scalar.activation(minus[:], silu_a1[q][:], SILU, scale=-1.0)
            nc.scalar.activation(silu_a1[q][:], silu_a1[q][:], SILU)
            tanh_a1[q], silu_minus_a1[q] = tanh_half, minus

        def times_sigmoid(q):
            nc.vector.scalar_tensor_tensor(factor[q][:], tanh_a1.pop(q)[:], 1.0, factor[q][:], ADD, MULT)

        def times_rest(q):
            nc.vector.scalar_tensor_tensor(factor[q][:], silu_minus_a1.pop(q)[:], 1.0, factor[q][:], SUB, MULT)

        def gather(j):
            rows = held.pop(("dyT", j))
            nc.vector.tensor_tensor(g[:, j, :], rows[:].indirect(offsets[:]), gate_rows[:], MULT)

        def round_g():
            round_into(True, *by_fours(g_grouped[:], g[:]))

        def quantize_g():
            quantize(g_codes[:], g_scales[:], g_grouped[:].rearrange("p c j -> p (c j)"))

        def round_w2(e):
            raw = held.pop(("w2", e))
            grouped = work.tile([P, H * J], BF16, name="w2_words", bufs=3, align_bytes=64)
            round_into(
                False,
                grouped[:].rearrange("p (t m j) -> p m j t", t=J, j=J),
                raw[:].rearrange("p j (m t) -> p m j t", t=J),
            )
            w2_grouped[e] = grouped

        def quantize_w2(e):
            codes = work.tile([P, H], U32, name="w2_codes", bufs=4, align_bytes=64)
            scales = work.tile([P, H], U8, name="w2_scales", bufs=4, align_bytes=64)
            quantize(codes[:], scales[:], w2_grouped.pop(e)[:])
            w2_packed[e] = (codes, scales)

        def first_product(e):
            packed = w2_packed.pop(e)
            dh = psum.tile([P, J, C], F32, name="dh")
            for t in range(J):
                multiply(dh[:, t, :], packed, slice(t * P, (t + 1) * P), (g_codes, g_scales), slice(e * C, (e + 1) * C), True, True)
            grouped = work.tile([P, 2, C, J], BF16, name="da_words", align_bytes=64)
            q, half = e // 2, slice((e % 2) * C, (e % 2 + 1) * C)
            nc.vector.scalar_tensor_tensor(
                grouped[:, 0, :, :],
                dh[:].rearrange("p r c -> p c r"),
                -0.5,
                factor[q][:, :, half].rearrange("p r c -> p c r"),
                MULT,
                MULT,
            )
            words, sums = by_fours(grouped[:, 1, :, :], dh[:])
            nc.vector.tensor_tensor(words, sums, silu_a1[q][:, :, half].rearrange("p r (c i) -> p c r i", i=4), MULT)
            da_grouped[e] = grouped

        def quantize_da(e):
            codes = work.tile([P, 2 * C], U32, name="da_codes", bufs=3, align_bytes=64)
            scales = work.tile([P, 2 * C], U8, name="da_scales", bufs=3, align_bytes=64)
            quantize(codes[:], scales[:], da_grouped.pop(e)[:].rearrange("p a c r -> p (a c r)"))
            da_packed[e] = (codes, scales)

        def round_w13(e, part=0):
            first, last = row_tiles(e)[part]
            if part == 0:
                grouped = work.tile([P, 2 * K, J], BF16, name="w13_words", align_bytes=64)
                w13_grouped[e] = grouped
            width = (last - first) * P
            for i, name in enumerate(("w1", "w3")):
                raw = held[(name, e)]
                if last == KT:
                    held.pop((name, e))
                at = 2 * P * first + i * width
                round_into(
                    (name, e) in ON_VECTOR,
                    *by_fours(w13_grouped[e][:, at : at + width, :], raw[:, :, first * P : last * P]),
                )

        def quantize_w13(e, part=0):
            first, last = row_tiles(e)[part]
            if part == 0:
                codes = work.tile([P, 2 * K], U32, name="w13_codes", align_bytes=64)
                scales = work.tile([P, 2 * K], U8, name="w13_scales", align_bytes=64)
                w13_packed[e] = (codes, scales)
            at, end = 2 * P * first, 2 * P * last
            while at < end:
                upto = min(at + 512, end)
                quantize(
                    w13_packed[e][0][:, at:upto],
                    w13_packed[e][1][:, at:upto],
                    w13_grouped[e][:, at:upto, :].rearrange("p c j -> p (c j)"),
                )
                at = upto

        def second_product(e, part=0):
            first, last = row_tiles(e)[part]
            dx = psum.tile([P, last - first, C], F32, name="dx", bufs=4)
            for k in range(first, last):
                for i in range(2):
                    at = 2 * P * first + i * (last - first) * P + (k - first) * P
                    multiply(dx[:, k - first, :], w13_packed[e], slice(at, at + P), da_packed[e], slice(i * C, (i + 1) * C), i == 0, i == 1)
            dx_banks[(e, part)] = dx

        def copy_dx(e, part=0):
            first, last = row_tiles(e)[part]
            if e // 2 not in dx_pairs:
                dx_pair = work.tile([P, KT, PAIR], F32, name="dx_pair")
                dx_pairs[e // 2] = dx_pair
            half = slice((e % 2) * C, (e % 2 + 1) * C)
            nc.scalar.copy(dx_pairs[e // 2][:, first:last, half], dx_banks.pop((e, part))[:])

        def scatter(q, k):
            columns = slice(q * PAIR // 16, (q + 1) * PAIR // 16)
            nc.vector.tensor_copy(results[k][:].indirect(offsets[:, columns]), dx_pairs[q][:, k, :])

        def store(k):
            nc.sync.dma_start(out[k * P : (k + 1) * P, :], results[k][:])

        of_pair = (activate, times_sigmoid, times_rest)
        pair_steps = [
            (quantize_da, 0, 2),
            (round_w2, 0, 0),
            (round_w13, 0, 1),
            (activate, 0, 0),
            (round_w2, 1, 0),
            (times_sigmoid, 0, 0),
            (quantize_w13, 1, 2),
            (quantize_w2, 0, 0),
            (scatter, 0, 3),
            (second_product, 0, 2),
            (quantize_w2, 1, 0),
            (first_product, 0, 1),
            (scatter, 1, 3),
            (copy_dx, 0, 2),
            (quantize_da, 1, 1),
            (second_product, 1, 2),
            (times_rest, 0, 0),
            (copy_dx, 1, 2),
            (round_w13, 1, 1),
            (first_product, 1, 0),
            (quantize_w13, 0, 1),
            (scatter, 2, 3),
        ]
        steps = [(gather, j) for j in range(J)] + [(round_g,), (quantize_g,)]
        for s in range(PAIRS + max(lag for function, member, lag in pair_steps)):
            for function, member, lag in pair_steps:
                q = s - lag
                if not 0 <= q < PAIRS:
                    continue
                if function in of_pair:
                    steps.append((function, q))
                elif function is scatter:
                    steps.append((function, q, member))
                else:
                    steps.append((function, 2 * q + member))
        late = (scatter, PAIRS - 1, KT - 1)
        steps.remove(late)
        for e in (E - 2, E - 1):
            steps += [(function, e, 1) for function in (round_w13, quantize_w13, second_product, copy_dx)]
        steps.append(late)
        steps += [(store, k) for k in range(KT)]
        for step in steps:
            load_ahead()
            step[0](*step[1:])
